import numpy as np
import ml_dtypes


def mxq(x, axis, fmt="e4m3"):
    dtype, down = {"e4m3": (ml_dtypes.float8_e4m3fn, 7), "e5m2": (ml_dtypes.float8_e5m2, 14)}[fmt]
    v = np.moveaxis(np.asarray(x, np.float32).astype(ml_dtypes.bfloat16).astype(np.float64), axis, -1)
    blocks = v.reshape(v.shape[:-1] + (-1, 32))
    amax = np.abs(blocks).max(-1, keepdims=True)
    byte = np.maximum(np.where(amax > 0, np.frexp(amax)[1] - 1 + 127, 0) - down, 1)
    scale = np.exp2(byte - 127.0)
    codes = (blocks / scale).astype(np.float32).astype(dtype).astype(np.float64)
    return np.moveaxis((codes * scale).reshape(v.shape), -1, axis)


WIDE = False


def mx_kscale(k):
    if not WIDE:
        return np.ones(k)
    levels = np.array([10, -10, 5, -5, 0])
    if k % 512:
        return np.exp2(np.random.permutation(np.resize(levels, k // 32))).repeat(32)
    a = np.empty((k // 512, 16))
    for p in range(k // 512):
        a[p, :8] = np.random.permutation(np.resize(levels, 8))
        for g in range(8):
            far = levels[np.abs(levels - a[p, g]) >= 10]
            a[p, g + 8] = far[np.random.randint(len(far))]
    return np.exp2(a.ravel()).repeat(32)


def f64(x):
    return np.asarray(x).astype(np.float64)


def striped(idx):
    return np.tile(np.asarray(idx).reshape(-1, 16).T, (8, 1)).astype(np.uint16)


def unstriped(offs):
    return offs[:16].T.reshape(-1).astype(np.int64)


G, K, T, D, M = 128, 4, 1024, 512, 256


def setup_inputs():
    n = np.random.standard_normal
    s = mx_kscale(D)[:, None]
    x = n((D, T)) * s
    idx = np.random.permutation(T)[:G * K].reshape(G, K)
    return {
        "xT": x.astype(np.float32),
        "w": (n((D, M)) / np.sqrt(D) / s).astype(np.float32),
        "bias": (0.3 * n((M, 1))).astype(np.float32),
        "offs": striped(idx.reshape(-1)),
    }


def reference(xT, w, bias, offs):
    x = f64(xT)[:, unstriped(offs)]
    y = (mxq(f64(w), 0, "e4m3").T @ mxq(x, 0, "e4m3")).reshape(M, G, K).max(-1)
    y = y + f64(bias)
    return y

@@ -1,0 +1,119 @@
+import concourse.mybir as mybir
+
+F32 = mybir.dt.float32
+BF16 = mybir.dt.bfloat16
+U32 = mybir.dt.uint32
+U16 = mybir.dt.uint16
+U8 = mybir.dt.uint8
+FP8X4 = mybir.dt.float8_e4m3fn_x4
+COPY = mybir.ActivationFunctionType.Copy
+IDENTITY = mybir.ActivationFunctionType.Identity
+MAX = mybir.AluOpType.max
+AXIS_X = mybir.AxisListType.X
+
+P = 128
+PACK = 4
+G, K, T, D, M = 128, 4, 1024, 512, 256
+N = G * K
+FLOPS = 2 * D * M * N
+
+
+def tile_attend_edge_uniq_bias_kernel(tc, xT, w, bias, offs, out):
+    nc = tc.nc
+    x_rows = xT.rearrange("(p t) c -> p t c", t=PACK)
+    w_rows = w.rearrange("(p t) m -> p t m", t=PACK)
+    out_rows = out.rearrange("(p h) g -> p h g", h=2)
+    half = N // 2
+    half_g = G // 2
+
+    with (
+        tc.tile_pool(name="held", bufs=1) as held,
+        tc.psum_pool(name="psum", bufs=1) as psum,
+    ):
+        offsets = held.tile([P, N // 16], U16, name="offsets")
+        raw_a = held.tile([P, 2, T], F32, name="raw_a", align_bytes=64)
+        raw_b = held.tile([P, 2, T], F32, name="raw_b", align_bytes=64)
+        raw_w = held.tile([P, PACK, M], F32, name="raw_w", align_bytes=64)
+        bias_cols = held.tile([P, 2], F32, name="bias_cols")
+
+        nc.sync.dma_start(raw_a[:, :, 0:512], x_rows[:, 0:2, 0:512])
+        nc.sync.dma_start(offsets[:], offs)
+        nc.sync.dma_start(raw_a[:, :, 512:1024], x_rows[:, 0:2, 512:1024])
+        nc.sync.dma_start(raw_b[:, :, 0:512], x_rows[:, 2:4, 0:512])
+        nc.sync.dma_start(raw_b[:, :, 512:768], x_rows[:, 2:4, 512:768])
+        nc.sync.dma_start(raw_b[:, :, 768:1024], x_rows[:, 2:4, 768:1024])
+        nc.sync.dma_start(raw_w[:, :, 0:128], w_rows[:, :, 0:128])
+        nc.sync.dma_start(raw_w[:, :, 128:256], w_rows[:, :, 128:256])
+        nc.sync.dma_start(bias_cols[:], bias.rearrange("(p h) o -> p (h o)", h=2))
+
+        pair_a = held.tile([P, T, 2], BF16, name="pair_a", align_bytes=64)
+        pair_b = held.tile([P, T, 2], BF16, name="pair_b", align_bytes=64)
+        w_grouped = held.tile([P, 2, P, PACK], BF16, name="w_grouped", align_bytes=64)
+        x_grouped = held.tile([P, N, PACK], BF16, name="x_grouped", align_bytes=64)
+        x_codes = held.tile([P, N], U32, name="x_codes", align_bytes=64)
+        x_scales = held.tile([P, N], U8, name="x_scales", align_bytes=64)
+        w_codes = held.tile([P, M], U32, name="w_codes", align_bytes=64)
+        w_scales = held.tile([P, M], U8, name="w_scales", align_bytes=64)
+
+        def pair_view(raw, lo, hi):
+            return raw[:, :, lo:hi].rearrange("p t c -> p c t")
+
+        a_words = pair_a[:].rearrange("p c t -> p (c t)").bitcast(U32)
+        b_words = pair_b[:].rearrange("p c t -> p (c t)").bitcast(U32)
+        x_words = x_grouped[:].rearrange("p c t -> p (c t)").bitcast(U32).rearrange("p (c u) -> p c u", u=2)
+        x_flat = x_grouped[:].rearrange("p c t -> p (c t)")
+
+        nc.scalar.activation(pair_a[:, 0:512, :], pair_view(raw_a, 0, 512), COPY)
+        nc.vector.tensor_copy(pair_a[:, 512:1024, :], pair_view(raw_a, 512, 1024))
+        nc.vector.tensor_copy(x_words[:, :, 0], a_words.indirect(offsets[:]))
+        nc.scalar.activation(pair_b[:, 0:512, :], pair_view(raw_b, 0, 512), COPY)
+        nc.vector.tensor_copy(pair_b[:, 512:768, :], pair_view(raw_b, 512, 768))
+        nc.vector.tensor_copy(pair_b[:, 768:1024, :], pair_view(raw_b, 768, 1024))
+        for q in range(2):
+            nc.scalar.activation(
+                w_grouped[:, :, 64 * q : 64 * q + 64, :],
+                raw_w[:, :, 128 * q : 128 * q + 128].rearrange("p t (m h) -> p h m t", h=2),
+                COPY,
+            )
+        for i in range(2):
+            nc.vector.tensor_copy(
+                x_words[:, half * i : half * i + half, 1],
+                b_words.indirect(offsets[:, 16 * i : 16 * i + 16]),
+            )
+        nc.vector.quantize_mx(x_codes[:, 0:half].bitcast(FP8X4), x_scales[:, 0:half], x_flat[:, 0 : 4 * half])
+        nc.vector.quantize_mx(w_codes[:].bitcast(FP8X4), w_scales[:], w_grouped[:].rearrange("p h m t -> p (h m t)"))
+        nc.vector.quantize_mx(x_codes[:, half:N].bitcast(FP8X4), x_scales[:, half:N], x_flat[:, 4 * half : 4 * N])
+
+        def multiply(acc, h, i):
+            nc.tensor.matmul_mx(
+                out=acc,
+                lhsT=w_codes[:, P * h : P * h + P].bitcast(FP8X4),
+                lhsT_scale=w_scales[:, P * h : P * h + P],
+                rhs=x_codes[:, half * i : half * i + half].bitcast(FP8X4),
+                rhs_scale=x_scales[:, half * i : half * i + half],
+                start=True,
+                stop=True,
+            )
+
+        acc_0 = psum.tile([P, 2, half], F32, name="acc_0")
+        top_0 = held.tile([P, 2, half_g], F32, name="top_0")
+        res_0 = held.tile([P, 2, half_g], F32, name="res_0")
+        top_1 = held.tile([P, 2, half_g], F32, name="top_1")
+        res_1 = held.tile([P, 2, half_g], F32, name="res_1")
+        for h in range(2):
+            multiply(acc_0[:, h, :], h, 0)
+        acc_1 = []
+        for h in range(2):
+            acc = psum.tile([P, half], F32, name=f"acc_1{h}")
+            multiply(acc[:], h, 1)
+            acc_1.append(acc)
+        nc.vector.tensor_reduce(
+            top_0[:].rearrange("p h g -> p (h g)"), acc_0[:].rearrange("p h (g j) -> p (h g) j", j=K), AXIS_X, MAX
+        )
+        for h in range(2):
+            nc.scalar.activation(res_0[:, h, :], top_0[:, h, :], IDENTITY, bias=bias_cols[:, h : h + 1])
+        nc.sync.dma_start(out_rows[:, :, 0:half_g], res_0[:])
+        for h in range(2):
+            nc.vector.tensor_reduce(top_1[:, h, :], acc_1[h][:].rearrange("p (g j) -> p g j", j=K), AXIS_X, MAX)
+            nc.scalar.activation(res_1[:, h, :], top_1[:, h, :], IDENTITY, bias=bias_cols[:, h : h + 1])
+        nc.sync.dma_start(out_rows[:, :, half_g:G], res_1[:])

@@ -36,14 +36,13 @@ def tile_attend_edge_uniq_bias_kernel(tc, xT, w, bias, offs, out):
         raw_w = held.tile([P, PACK, M], F32, name="raw_w", align_bytes=64)
         bias_cols = held.tile([P, 2], F32, name="bias_cols")
 
-        nc.sync.dma_start(raw_a[:, :, 0:512], x_rows[:, 0:2, 0:512])
+        nc.sync.dma_start(raw_a[:, :, 0:768], x_rows[:, 0:2, 0:768])
         nc.sync.dma_start(offsets[:], offs)
-        nc.sync.dma_start(raw_a[:, :, 512:1024], x_rows[:, 0:2, 512:1024])
+        nc.sync.dma_start(raw_a[:, :, 768:1024], x_rows[:, 0:2, 768:1024])
         nc.sync.dma_start(raw_b[:, :, 0:512], x_rows[:, 2:4, 0:512])
-        nc.sync.dma_start(raw_b[:, :, 512:768], x_rows[:, 2:4, 512:768])
-        nc.sync.dma_start(raw_b[:, :, 768:1024], x_rows[:, 2:4, 768:1024])
-        nc.sync.dma_start(raw_w[:, :, 0:128], w_rows[:, :, 0:128])
-        nc.sync.dma_start(raw_w[:, :, 128:256], w_rows[:, :, 128:256])
+        nc.sync.dma_start(raw_b[:, :, 512:832], x_rows[:, 2:4, 512:832])
+        nc.sync.dma_start(raw_b[:, :, 832:1024], x_rows[:, 2:4, 832:1024])
+        nc.sync.dma_start(raw_w[:], w_rows)
         nc.sync.dma_start(bias_cols[:], bias.rearrange("(p h) o -> p (h o)", h=2))
 
         pair_a = held.tile([P, T, 2], BF16, name="pair_a", align_bytes=64)
@@ -63,12 +62,21 @@ def tile_attend_edge_uniq_bias_kernel(tc, xT, w, bias, offs, out):
         x_words = x_grouped[:].rearrange("p c t -> p (c t)").bitcast(U32).rearrange("p (c u) -> p c u", u=2)
         x_flat = x_grouped[:].rearrange("p c t -> p (c t)")
 
-        nc.scalar.activation(pair_a[:, 0:512, :], pair_view(raw_a, 0, 512), COPY)
-        nc.vector.tensor_copy(pair_a[:, 512:1024, :], pair_view(raw_a, 512, 1024))
+        def cast_v(pair, raw, lo, hi):
+            nc.vector.tensor_copy(pair[:, lo:hi, :], pair_view(raw, lo, hi))
+
+        def cast_s(pair, raw, lo, hi):
+            nc.scalar.activation(pair[:, lo:hi, :], pair_view(raw, lo, hi), COPY)
+
+        cast_v(pair_a, raw_a, 0, 512)
+        cast_s(pair_a, raw_a, 512, 768)
+        cast_v(pair_a, raw_a, 768, 936)
+        cast_s(pair_a, raw_a, 936, 1024)
         nc.vector.tensor_copy(x_words[:, :, 0], a_words.indirect(offsets[:]))
-        nc.scalar.activation(pair_b[:, 0:512, :], pair_view(raw_b, 0, 512), COPY)
-        nc.vector.tensor_copy(pair_b[:, 512:768, :], pair_view(raw_b, 512, 768))
-        nc.vector.tensor_copy(pair_b[:, 768:1024, :], pair_view(raw_b, 768, 1024))
+        cast_s(pair_b, raw_b, 0, 512)
+        cast_v(pair_b, raw_b, 512, 832)
+        cast_v(pair_b, raw_b, 832, 944)
+        cast_s(pair_b, raw_b, 944, 1024)
         for q in range(2):
             nc.scalar.activation(
                 w_grouped[:, :, 64 * q : 64 * q + 64, :],
@@ -95,25 +103,15 @@ def tile_attend_edge_uniq_bias_kernel(tc, xT, w, bias, offs, out):
                 stop=True,
             )
 
-        acc_0 = psum.tile([P, 2, half], F32, name="acc_0")
-        top_0 = held.tile([P, 2, half_g], F32, name="top_0")
-        res_0 = held.tile([P, 2, half_g], F32, name="res_0")
-        top_1 = held.tile([P, 2, half_g], F32, name="top_1")
-        res_1 = held.tile([P, 2, half_g], F32, name="res_1")
-        for h in range(2):
-            multiply(acc_0[:, h, :], h, 0)
-        acc_1 = []
-        for h in range(2):
-            acc = psum.tile([P, half], F32, name=f"acc_1{h}")
-            multiply(acc[:], h, 1)
-            acc_1.append(acc)
-        nc.vector.tensor_reduce(
-            top_0[:].rearrange("p h g -> p (h g)"), acc_0[:].rearrange("p h (g j) -> p (h g) j", j=K), AXIS_X, MAX
-        )
-        for h in range(2):
-            nc.scalar.activation(res_0[:, h, :], top_0[:, h, :], IDENTITY, bias=bias_cols[:, h : h + 1])
-        nc.sync.dma_start(out_rows[:, :, 0:half_g], res_0[:])
-        for h in range(2):
-            nc.vector.tensor_reduce(top_1[:, h, :], acc_1[h][:].rearrange("p (g j) -> p g j", j=K), AXIS_X, MAX)
-            nc.scalar.activation(res_1[:, h, :], top_1[:, h, :], IDENTITY, bias=bias_cols[:, h : h + 1])
-        nc.sync.dma_start(out_rows[:, :, half_g:G], res_1[:])
+        for i in range(2):
+            top = held.tile([P, 2, half_g], F32, name=f"top_{i}")
+            res = held.tile([P, 2, half_g], F32, name=f"res_{i}")
+            accs = []
+            for h in range(2):
+                acc = psum.tile([P, half], F32, name=f"acc_{i}{h}")
+                multiply(acc[:], h, i)
+                accs.append(acc)
+            for h in range(2):
+                nc.vector.tensor_reduce(top[:, h, :], accs[h][:].rearrange("p (g j) -> p g j", j=K), AXIS_X, MAX)
+                nc.scalar.activation(res[:, h, :], top[:, h, :], IDENTITY, bias=bias_cols[:, h : h + 1])
+            nc.sync.dma_start(out_rows[:, :, half_g * i : half_g * i + half_g], res[:])

@@ -37,8 +37,8 @@ def tile_attend_edge_uniq_bias_kernel(tc, xT, w, bias, offs, out):
         bias_cols = held.tile([P, 2], F32, name="bias_cols")
 
         nc.sync.dma_start(raw_a[:, :, 0:768], x_rows[:, 0:2, 0:768])
-        nc.sync.dma_start(offsets[:], offs)
         nc.sync.dma_start(raw_a[:, :, 768:1024], x_rows[:, 0:2, 768:1024])
+        nc.sync.dma_start(offsets[:], offs)
         nc.sync.dma_start(raw_b[:, :, 0:512], x_rows[:, 2:4, 0:512])
         nc.sync.dma_start(raw_b[:, :, 512:832], x_rows[:, 2:4, 512:832])
         nc.sync.dma_start(raw_b[:, :, 832:1024], x_rows[:, 2:4, 832:1024])
@@ -77,41 +77,62 @@ def tile_attend_edge_uniq_bias_kernel(tc, xT, w, bias, offs, out):
         cast_v(pair_b, raw_b, 512, 832)
         cast_v(pair_b, raw_b, 832, 944)
         cast_s(pair_b, raw_b, 944, 1024)
-        for q in range(2):
-            nc.scalar.activation(
-                w_grouped[:, :, 64 * q : 64 * q + 64, :],
-                raw_w[:, :, 128 * q : 128 * q + 128].rearrange("p t (m h) -> p h m t", h=2),
-                COPY,
-            )
+        for h in range(2):
+            nc.scalar.activation(w_grouped[:, h, :, :], raw_w[:].rearrange("p t (m h) -> p h m t", h=2)[:, h, :, :], COPY)
         for i in range(2):
             nc.vector.tensor_copy(
                 x_words[:, half * i : half * i + half, 1],
                 b_words.indirect(offsets[:, 16 * i : 16 * i + 16]),
             )
         nc.vector.quantize_mx(x_codes[:, 0:half].bitcast(FP8X4), x_scales[:, 0:half], x_flat[:, 0 : 4 * half])
-        nc.vector.quantize_mx(w_codes[:].bitcast(FP8X4), w_scales[:], w_grouped[:].rearrange("p h m t -> p (h m t)"))
+        for h in range(2):
+            nc.vector.quantize_mx(
+                w_codes[:, P * h : P * h + P].bitcast(FP8X4),
+                w_scales[:, P * h : P * h + P],
+                w_grouped[:, h, :, :].rearrange("p m t -> p (m t)"),
+            )
         nc.vector.quantize_mx(x_codes[:, half:N].bitcast(FP8X4), x_scales[:, half:N], x_flat[:, 4 * half : 4 * N])
 
-        def multiply(acc, h, i):
+        def multiply(h, lo, hi):
+            acc = psum.tile([P, hi - lo], F32, name=f"acc_{h}_{lo}")
             nc.tensor.matmul_mx(
-                out=acc,
+                out=acc[:],
                 lhsT=w_codes[:, P * h : P * h + P].bitcast(FP8X4),
                 lhsT_scale=w_scales[:, P * h : P * h + P],
-                rhs=x_codes[:, half * i : half * i + half].bitcast(FP8X4),
-                rhs_scale=x_scales[:, half * i : half * i + half],
+                rhs=x_codes[:, lo:hi].bitcast(FP8X4),
+                rhs_scale=x_scales[:, lo:hi],
                 start=True,
                 stop=True,
             )
+            return acc
 
+        def largest(top, acc):
+            nc.vector.tensor_reduce(top, acc[:].rearrange("p (g j) -> p g j", j=K), AXIS_X, MAX)
+
+        def add_bias(res, top, h):
+            nc.scalar.activation(res, top, IDENTITY, bias=bias_cols[:, h : h + 1])
+
+        acc_00 = multiply(0, 0, 256)
+        acc_10 = multiply(1, 0, 256)
+        acc_01 = multiply(0, 256, 512)
+        acc_11 = multiply(1, 256, 384)
+        acc_12 = multiply(1, 384, 512)
+        tops = []
+        ress = []
         for i in range(2):
             top = held.tile([P, 2, half_g], F32, name=f"top_{i}")
             res = held.tile([P, 2, half_g], F32, name=f"res_{i}")
-            accs = []
-            for h in range(2):
-                acc = psum.tile([P, half], F32, name=f"acc_{i}{h}")
-                multiply(acc[:], h, i)
-                accs.append(acc)
-            for h in range(2):
-                nc.vector.tensor_reduce(top[:, h, :], accs[h][:].rearrange("p (g j) -> p g j", j=K), AXIS_X, MAX)
-                nc.scalar.activation(res[:, h, :], top[:, h, :], IDENTITY, bias=bias_cols[:, h : h + 1])
-            nc.sync.dma_start(out_rows[:, :, half_g * i : half_g * i + half_g], res[:])
+            tops.append(top)
+            ress.append(res)
+        largest(tops[0][:, 0, :], acc_00)
+        add_bias(ress[0][:, 0, :], tops[0][:, 0, :], 0)
+        largest(tops[0][:, 1, :], acc_10)
+        add_bias(ress[0][:, 1, :], tops[0][:, 1, :], 1)
+        nc.sync.dma_start(out_rows[:, :, 0:half_g], ress[0][:])
+        largest(tops[1][:, 0, :], acc_01)
+        add_bias(ress[1][:, 0, :], tops[1][:, 0, :], 0)
+        nc.sync.dma_start(out_rows[:, 0, half_g:G], ress[1][:, 0, :])
+        largest(tops[1][:, 1, 0:32], acc_11)
+        largest(tops[1][:, 1, 32:64], acc_12)
+        add_bias(ress[1][:, 1, :], tops[1][:, 1, :], 1)
+        nc.sync.dma_start(out_rows[:, 1, half_g:G], ress[1][:, 1, :])

import concourse.mybir as mybir

F32 = mybir.dt.float32
BF16 = mybir.dt.bfloat16
U32 = mybir.dt.uint32
U16 = mybir.dt.uint16
U8 = mybir.dt.uint8
FP8X4 = mybir.dt.float8_e4m3fn_x4
COPY = mybir.ActivationFunctionType.Copy
IDENTITY = mybir.ActivationFunctionType.Identity
MAX = mybir.AluOpType.max
AXIS_X = mybir.AxisListType.X

P = 128
PACK = 4
G, K, T, D, M = 128, 4, 1024, 512, 256
N = G * K
FLOPS = 2 * D * M * N


def tile_attend_edge_uniq_bias_kernel(tc, xT, w, bias, offs, out):
    nc = tc.nc
    x_rows = xT.rearrange("(p t) c -> p t c", t=PACK)
    w_rows = w.rearrange("(p t) m -> p t m", t=PACK)
    out_rows = out.rearrange("(p h) g -> p h g", h=2)
    half = N // 2
    half_g = G // 2

    with (
        tc.tile_pool(name="held", bufs=1) as held,
        tc.psum_pool(name="psum", bufs=1) as psum,
    ):
        offsets = held.tile([P, N // 16], U16, name="offsets")
        raw_a = held.tile([P, 2, T], F32, name="raw_a", align_bytes=64)
        raw_b = held.tile([P, 2, T], F32, name="raw_b", align_bytes=64)
        raw_w = held.tile([P, PACK, M], F32, name="raw_w", align_bytes=64)
        bias_cols = held.tile([P, 2], F32, name="bias_cols")

        nc.sync.dma_start(raw_a[:, :, 0:768], x_rows[:, 0:2, 0:768])
        nc.sync.dma_start(raw_a[:, :, 768:1024], x_rows[:, 0:2, 768:1024])
        nc.sync.dma_start(offsets[:], offs)
        nc.sync.dma_start(raw_b[:, :, 0:512], x_rows[:, 2:4, 0:512])
        nc.sync.dma_start(raw_b[:, :, 512:832], x_rows[:, 2:4, 512:832])
        nc.sync.dma_start(raw_b[:, :, 832:1024], x_rows[:, 2:4, 832:1024])
        nc.sync.dma_start(raw_w[:], w_rows)
        nc.sync.dma_start(bias_cols[:], bias.rearrange("(p h) o -> p (h o)", h=2))

        pair_a = held.tile([P, T, 2], BF16, name="pair_a", align_bytes=64)
        pair_b = held.tile([P, T, 2], BF16, name="pair_b", align_bytes=64)
        w_grouped = held.tile([P, 2, P, PACK], BF16, name="w_grouped", align_bytes=64)
        x_grouped = held.tile([P, N, PACK], BF16, name="x_grouped", align_bytes=64)
        x_codes = held.tile([P, N], U32, name="x_codes", align_bytes=64)
        x_scales = held.tile([P, N], U8, name="x_scales", align_bytes=64)
        w_codes = held.tile([P, M], U32, name="w_codes", align_bytes=64)
        w_scales = held.tile([P, M], U8, name="w_scales", align_bytes=64)

        def pair_view(raw, lo, hi):
            return raw[:, :, lo:hi].rearrange("p t c -> p c t")

        a_words = pair_a[:].rearrange("p c t -> p (c t)").bitcast(U32)
        b_words = pair_b[:].rearrange("p c t -> p (c t)").bitcast(U32)
        x_words = x_grouped[:].rearrange("p c t -> p (c t)").bitcast(U32).rearrange("p (c u) -> p c u", u=2)
        x_flat = x_grouped[:].rearrange("p c t -> p (c t)")

        def cast_v(pair, raw, lo, hi):
            nc.vector.tensor_copy(pair[:, lo:hi, :], pair_view(raw, lo, hi))

        def cast_s(pair, raw, lo, hi):
            nc.scalar.activation(pair[:, lo:hi, :], pair_view(raw, lo, hi), COPY)

        cast_v(pair_a, raw_a, 0, 512)
        cast_s(pair_a, raw_a, 512, 768)
        cast_v(pair_a, raw_a, 768, 936)
        cast_s(pair_a, raw_a, 936, 1024)
        nc.vector.tensor_copy(x_words[:, :, 0], a_words.indirect(offsets[:]))
        cast_s(pair_b, raw_b, 0, 512)
        cast_v(pair_b, raw_b, 512, 832)
        cast_v(pair_b, raw_b, 832, 944)
        cast_s(pair_b, raw_b, 944, 1024)
        for h in range(2):
            nc.scalar.activation(w_grouped[:, h, :, :], raw_w[:].rearrange("p t (m h) -> p h m t", h=2)[:, h, :, :], COPY)
        for i in range(2):
            nc.vector.tensor_copy(
                x_words[:, half * i : half * i + half, 1],
                b_words.indirect(offsets[:, 16 * i : 16 * i + 16]),
            )
        nc.vector.quantize_mx(x_codes[:, 0:half].bitcast(FP8X4), x_scales[:, 0:half], x_flat[:, 0 : 4 * half])
        for h in range(2):
            nc.vector.quantize_mx(
                w_codes[:, P * h : P * h + P].bitcast(FP8X4),
                w_scales[:, P * h : P * h + P],
                w_grouped[:, h, :, :].rearrange("p m t -> p (m t)"),
            )
        nc.vector.quantize_mx(x_codes[:, half:N].bitcast(FP8X4), x_scales[:, half:N], x_flat[:, 4 * half : 4 * N])

        def multiply(h, lo, hi):
            acc = psum.tile([P, hi - lo], F32, name=f"acc_{h}_{lo}")
            nc.tensor.matmul_mx(
                out=acc[:],
                lhsT=w_codes[:, P * h : P * h + P].bitcast(FP8X4),
                lhsT_scale=w_scales[:, P * h : P * h + P],
                rhs=x_codes[:, lo:hi].bitcast(FP8X4),
                rhs_scale=x_scales[:, lo:hi],
                start=True,
                stop=True,
            )
            return acc

        def largest(top, acc):
            nc.vector.tensor_reduce(top, acc[:].rearrange("p (g j) -> p g j", j=K), AXIS_X, MAX)

        def add_bias(res, top, h):
            nc.scalar.activation(res, top, IDENTITY, bias=bias_cols[:, h : h + 1])

        acc_00 = multiply(0, 0, 256)
        acc_10 = multiply(1, 0, 256)
        acc_01 = multiply(0, 256, 512)
        acc_11 = multiply(1, 256, 384)
        acc_12 = multiply(1, 384, 512)
        tops = []
        ress = []
        for i in range(2):
            top = held.tile([P, 2, half_g], F32, name=f"top_{i}")
            res = held.tile([P, 2, half_g], F32, name=f"res_{i}")
            tops.append(top)
            ress.append(res)
        largest(tops[0][:, 0, :], acc_00)
        add_bias(ress[0][:, 0, :], tops[0][:, 0, :], 0)
        largest(tops[0][:, 1, :], acc_10)
        add_bias(ress[0][:, 1, :], tops[0][:, 1, :], 1)
        nc.sync.dma_start(out_rows[:, :, 0:half_g], ress[0][:])
        largest(tops[1][:, 0, :], acc_01)
        add_bias(ress[1][:, 0, :], tops[1][:, 0, :], 0)
        nc.sync.dma_start(out_rows[:, 0, half_g:G], ress[1][:, 0, :])
        largest(tops[1][:, 1, 0:32], acc_11)
        largest(tops[1][:, 1, 32:64], acc_12)
        add_bias(ress[1][:, 1, :], tops[1][:, 1, :], 1)
        nc.sync.dma_start(out_rows[:, 1, half_g:G], ress[1][:, 1, :])
